import numpy as np
import ml_dtypes


def mxq(x, axis, fmt="e4m3"):
    dtype, down = {"e4m3": (ml_dtypes.float8_e4m3fn, 7), "e5m2": (ml_dtypes.float8_e5m2, 14)}[fmt]
    v = np.moveaxis(np.asarray(x, np.float32).astype(ml_dtypes.bfloat16).astype(np.float64), axis, -1)
    blocks = v.reshape(v.shape[:-1] + (-1, 32))
    amax = np.abs(blocks).max(-1, keepdims=True)
    byte = np.maximum(np.where(amax > 0, np.frexp(amax)[1] - 1 + 127, 0) - down, 1)
    scale = np.exp2(byte - 127.0)
    codes = (blocks / scale).astype(np.float32).astype(dtype).astype(np.float64)
    return np.moveaxis((codes * scale).reshape(v.shape), -1, axis)


WIDE = False


def mx_kscale(k):
    if not WIDE:
        return np.ones(k)
    levels = np.array([10, -10, 5, -5, 0])
    if k % 512:
        return np.exp2(np.random.permutation(np.resize(levels, k // 32))).repeat(32)
    a = np.empty((k // 512, 16))
    for p in range(k // 512):
        a[p, :8] = np.random.permutation(np.resize(levels, 8))
        for g in range(8):
            far = levels[np.abs(levels - a[p, g]) >= 10]
            a[p, g + 8] = far[np.random.randint(len(far))]
    return np.exp2(a.ravel()).repeat(32)


def f64(x):
    return np.asarray(x).astype(np.float64)


def striped(idx):
    return np.tile(idx.reshape(-1, 16).T, (8, 1)).astype(np.uint16)


def unstriped(offs):
    return offs[:16].T.reshape(-1).astype(np.int64)


E2M1 = np.array([0.0, 0.5, 1.0, 1.5, 2.0, 3.0, 4.0, 6.0, -0.0, -0.5, -1.0, -1.5, -2.0, -3.0, -4.0, -6.0])


def pack_weight(w, fmt):
    k, n = w.shape
    w = f64(np.asarray(w, np.float32).astype(ml_dtypes.bfloat16)).reshape(k // 32, 32, n)
    amax = np.abs(w).max(1)
    if fmt == "e4m3":
        byte = np.frexp(amax)[1] - 1 + 127 - 7
    else:
        mant, ex = np.frexp(amax / 6.0)
        byte = np.where(mant > 0.5, ex, ex - 1) + 127
    byte = np.clip(np.where(amax > 0, byte, 1), 1, 254)
    scaled = (w * np.exp2(127.0 - byte)[:, None, :]).reshape(k, n).astype(np.float32)
    by_word = np.ascontiguousarray(scaled.reshape(k // 512, 128, 4, n).transpose(0, 1, 3, 2))
    if fmt == "e4m3":
        words = by_word.astype(ml_dtypes.float8_e4m3fn).view(np.uint8)
    else:
        c = by_word.astype(ml_dtypes.float4_e2m1fn).view(np.uint8) & 0xF
        words = (c[..., 0::2] | (c[..., 1::2] << 4)).reshape(k // 512, 128, 2 * n)
    return np.ascontiguousarray(words), np.ascontiguousarray(byte.astype(np.uint8).reshape(k // 512, 16, n))


def unpack_weight(words, scales, fmt):
    g, _, n = scales.shape
    words = np.ascontiguousarray(words).reshape(g, 128, n, -1)
    if fmt == "e4m3":
        vals = words.view(ml_dtypes.float8_e4m3fn).astype(np.float64)
    else:
        nib = np.empty((g, 128, n, 4), np.uint8)
        nib[..., 0::2] = words & 0xF
        nib[..., 1::2] = words >> 4
        vals = E2M1[nib]
    vals = vals * np.repeat(np.exp2(scales.astype(np.float64) - 127.0), 8, axis=1)[..., None]
    return vals.transpose(0, 1, 3, 2).reshape(g * 512, n)


def sigmoid(v):
    return 1.0 / (1.0 + np.exp(-np.maximum(v, -700.0)))


K, T, E, C, H, N = 512, 1024, 8, 256, 512, 256
TOP = 3
PAD = 64


def by_expert(wq, xq):
    return np.concatenate([wq[e].T @ xq[:, e * C:(e + 1) * C] for e in range(E)], axis=1)


def setup_inputs():
    n = np.random.standard_normal
    s = mx_kscale(K)[:, None]
    u = mx_kscale(H)
    slot_token = np.empty(E * C, np.int64); pos = np.tile(E * C + np.arange(T) % PAD, (TOP, 1)); taken = np.zeros(T, np.int64)
    liked = np.random.randn(T)
    for e in np.random.permutation(E):
        free = np.flatnonzero(taken < TOP); pick = np.random.permutation(free[np.argsort(-(liked[free] + np.random.gumbel(size=free.size)))[:C]]); slot_token[e * C:(e + 1) * C] = pick
        pos[taken[pick], pick] = e * C + np.arange(C); taken[pick] += 1
    g = np.random.uniform(0.2, 0.8, (TOP, T))
    x = pack_weight(n((K, T)) * s, "e4m3")
    return {
        "x_words": x[0],
        "x_scales": x[1],
        "w1": (n((E, K, H)) / np.sqrt(K) / s[None]).astype(np.float32),
        "w3": (n((E, K, H)) / np.sqrt(K) / s[None] * u[None, None, :]).astype(np.float32),
        "w2": (n((E, H, N)) / np.sqrt(H) / u[None, :, None]).astype(np.float32),
        "gate": np.stack([np.tile(r, (N, 1)) for r in g]).astype(np.float32),
        "offs": striped(slot_token),
        "pos1": striped(pos[0]),
        "pos2": striped(pos[1]),
        "pos3": striped(pos[2]),
    }


def reference(x_words, x_scales, w1, w3, w2, gate, offs, pos1, pos2, pos3):
    idx = unstriped(offs)
    xq = unpack_weight(x_words, x_scales, "e4m3")[:, idx]
    h = sigmoid(by_expert(mxq(f64(w1), 1, "e4m3"), xq))
    h = h * by_expert(mxq(f64(w3), 1, "e4m3"), xq)
    y = by_expert(mxq(f64(w2), 1, "e4m3"), mxq(h, 0, "e4m3"))
    y = np.concatenate([y, np.zeros((N, PAD))], axis=1)
    return sum(f64(gate[r]) * y[:, unstriped(p)] for r, p in enumerate((pos1, pos2, pos3)))

@@ -1,0 +1,207 @@
+from contextlib import ExitStack
+
+import concourse.mybir as mybir
+
+K, T, E, C, H, N = 512, 1024, 8, 256, 512, 256
+TOP = 3
+PAD = 64
+S = E * C
+
+FLOPS = 2 * S * (2 * K * H + H * N)
+BYTES = 4 * E * (2 * K * H + H * N) + K * T + 16 * T + 4 * TOP * T + 2 * (S + TOP * T) + 4 * N * T
+
+F32 = mybir.dt.float32
+BF16 = mybir.dt.bfloat16
+I32 = mybir.dt.int32
+U32 = mybir.dt.uint32
+U16 = mybir.dt.uint16
+U8 = mybir.dt.uint8
+FP8X4 = mybir.dt.float8_e4m3fn_x4
+MULT = mybir.AluOpType.mult
+ADD = mybir.AluOpType.add
+COPY = mybir.ActivationFunctionType.Copy
+SIGMOID = mybir.ActivationFunctionType.Sigmoid
+
+P = 128
+PACK = 4
+HALF = 128
+W2_LAG = 3
+CHUNK = 512
+V_M1 = 128
+V_M3 = 0
+V_C2 = 128
+
+
+def tile_moe_ecr_glu_sigmoid_kernel(tc, x_words, x_scales, w1, w3, w2, gate, offs, pos1, pos2, pos3, out):
+    nc = tc.nc
+    with ExitStack() as ctx:
+        keep = ctx.enter_context(tc.tile_pool(name="keep", bufs=1))
+        raw = ctx.enter_context(tc.tile_pool(name="raw", bufs=1))
+        work = ctx.enter_context(tc.tile_pool(name="work", bufs=2))
+        psum = ctx.enter_context(tc.psum_pool(name="psum", bufs=1))
+
+        offs_sb = keep.tile([P, S // 16], U16, name="offs_sb")
+        nc.sync.dma_start(offs_sb[:], offs)
+        xw = keep.tile([P, T], I32, name="xw", align_bytes=64)
+        nc.sync.dma_start(xw[:], x_words[0].rearrange("p t r -> p (t r)").bitcast(I32))
+        xs_rows = keep.tile([4, 4, T // 4], I32, name="xs_rows")
+        nc.sync.dma_start(xs_rows[:], x_scales[0].bitcast(I32).rearrange("(q r) w -> r q w", r=4))
+        xs = keep.tile([P, T], U8, name="xs", align_bytes=64)
+        nc.vector.memset(xs[:].bitcast(I32), 0)
+        for q in range(4):
+            nc.vector.tensor_copy(xs[32 * q : 32 * q + 4, :].bitcast(I32), xs_rows[:, q, :])
+
+        y = [keep.tile([P, S + PAD], F32, name=f"y{nb}") for nb in range(N // P)]
+        for nb in range(N // P):
+            nc.gpsimd.memset(y[nb][:, S:], 0.0)
+
+        xg_words = {}
+        xg_scales = {}
+
+        def gather_tokens(pair):
+            cols = offs_sb[:, pair * 2 * C // 16 : (pair + 1) * 2 * C // 16]
+            xg_words[pair] = work.tile([P, 2 * C], U32, name="xgw", align_bytes=64)
+            xg_scales[pair] = work.tile([P, 2 * C], U8, name="xgs", align_bytes=64)
+            nc.vector.tensor_copy(xg_words[pair][:], xw[:].bitcast(U32).indirect(cols))
+            nc.vector.tensor_copy(xg_scales[pair][:], xs[:].indirect(cols))
+
+        def load_first(w, e, name):
+            rows = w[e].rearrange("(p j) c -> p j c", j=PACK)
+            if e > 0:
+                t = raw.tile([P, PACK, H], F32, name=name, tag="raw13", bufs=10)
+                nc.sync.dma_start(t[:], rows)
+                return [t]
+            parts = []
+            for c0 in range(0, H, N):
+                t = raw.tile([P, PACK, N], F32, name=name + "_part", tag="raw2", bufs=6)
+                nc.sync.dma_start(t[:], rows[:, :, c0 : c0 + N])
+                parts.append(t)
+            return parts
+
+        def load_second(e):
+            t = raw.tile([P, PACK, N], F32, name="w2_raw", tag="raw2", bufs=6)
+            nc.sync.dma_start(t[:], w2[e].rearrange("(p j) n -> p j n", j=PACK))
+            return t
+
+        def quantize(src, width, name, bufs):
+            codes = work.tile([P, width], U32, name=name + "_codes", align_bytes=64, bufs=bufs)
+            scales = work.tile([P, width], U8, name=name + "_scales", align_bytes=64, bufs=bufs)
+            nc.vector.quantize_mx(out=codes[:].bitcast(FP8X4), scales=scales[:], in_=src[:])
+            return codes, scales
+
+        def round_first(w_raw, name, on_vector):
+            grouped = work.tile([P, PACK * H], BF16, name=name + "_bf", align_bytes=64)
+            dst = grouped[:].rearrange("p (t m j) -> p m j t", t=PACK, j=PACK)
+            if len(w_raw) > 1:
+                for i, part in enumerate(w_raw):
+                    m = P // len(w_raw)
+                    nc.scalar.copy(dst[:, i * m : (i + 1) * m], part[:].rearrange("p j (m t) -> p m j t", t=PACK))
+                return quantize(grouped, H, name, 2)
+            src = w_raw[0][:].rearrange("p j (m t) -> p m j t", t=PACK)
+            if on_vector > 0:
+                nc.vector.tensor_copy(dst[:, :on_vector], src[:, :on_vector])
+            if on_vector < P:
+                nc.scalar.copy(dst[:, on_vector:], src[:, on_vector:])
+            return quantize(grouped, H, name, 2)
+
+        def first_layer(e, w1_raw, w3_raw):
+            w3q = round_first(w3_raw, "w3", V_M3)
+            w1q = round_first(w1_raw, "w1", V_M1)
+            h = work.tile([P, C * PACK], BF16, name="h", align_bytes=64)
+            for half in range(C // HALF):
+                first = (e % 2) * C + half * HALF
+                slots = slice(first, first + HALF)
+                banks = []
+                for name, (codes, scales) in (("a", w1q), ("b", w3q)):
+                    bank = psum.tile([P, PACK, HALF], F32, name=name, bufs=3)
+                    for t in range(PACK):
+                        cols = slice(t * P, (t + 1) * P)
+                        nc.tensor.matmul_mx(
+                            out=bank[:, t, :],
+                            lhsT=codes[:, cols].bitcast(FP8X4),
+                            lhsT_scale=scales[:, cols],
+                            rhs=xg_words[e // 2][:, slots].bitcast(FP8X4),
+                            rhs_scale=xg_scales[e // 2][:, slots],
+                            start=True,
+                            stop=True,
+                        )
+                    banks.append(bank)
+                sig = work.tile([P, HALF, PACK], F32, name="sig", bufs=3)
+                nc.scalar.activation(sig[:], banks[0][:].rearrange("p t n -> p n t"), SIGMOID)
+                h_half = h[:, half * HALF * PACK : (half + 1) * HALF * PACK].rearrange("p (n t) -> p n t", t=PACK)
+                nc.vector.tensor_tensor(h_half, banks[1][:].rearrange("p t n -> p n t"), sig[:], MULT)
+            return quantize(h, C, "h", W2_LAG + 2)
+
+        def second_layer(e, w2_raw, hq):
+            grouped = work.tile([P, PACK * N], BF16, name="w2_bf", align_bytes=64)
+            src = w2_raw[:].rearrange("p j (c i) -> p c j i", i=4)
+            cut = V_C2 * PACK
+            nc.vector.tensor_copy(grouped[:, :cut].rearrange("p (c i j) -> p c j i", i=4, j=PACK), src[:, : V_C2 // 4])
+            nc.scalar.copy(grouped[:, cut:].rearrange("p (c i j) -> p c j i", i=4, j=PACK), src[:, V_C2 // 4 :])
+            codes, scales = quantize(grouped, N, "w2", 2)
+            bank = psum.tile([P, N // P, C], F32, name="ybank", bufs=2)
+            for nb in range(N // P):
+                cols = slice(nb * P, (nb + 1) * P)
+                nc.tensor.matmul_mx(
+                    out=bank[:, nb, :],
+                    lhsT=codes[:, cols].bitcast(FP8X4),
+                    lhsT_scale=scales[:, cols],
+                    rhs=hq[0][:].bitcast(FP8X4),
+                    rhs_scale=hq[1][:],
+                    start=True,
+                    stop=True,
+                )
+            for nb in range(N // P):
+                nc.scalar.copy(y[nb][:, e * C : (e + 1) * C], bank[:, nb, :])
+
+        hq = {}
+        for step in range(E + W2_LAG):
+            e2 = step - W2_LAG
+            if step < E:
+                w3_raw = load_first(w3, step, "w3_raw")
+                w1_raw = load_first(w1, step, "w1_raw")
+            if e2 >= 0:
+                w2_raw = load_second(e2)
+            if step < E:
+                if step % 2 == 0:
+                    gather_tokens(step // 2)
+                hq[step] = first_layer(step, w1_raw, w3_raw)
+            if e2 >= 0:
+                second_layer(e2, w2_raw, hq[e2])
+
+        lists = []
+        gates = []
+        for r, pos in enumerate((pos1, pos2, pos3)):
+            pos_sb = keep.tile([P, T // 16], U16, name=f"pos{r}")
+            nc.sync.dma_start(pos_sb[:], pos)
+            lists.append(pos_sb)
+            g = raw.tile([P, T], F32, name=f"gate{r}", tag="raw2", bufs=6)
+            nc.sync.dma_start(g[:], gate[r, 0:P, :])
+            gates.append(g)
+
+        units = [(nb, t0) for nb in range(N // P) for t0 in range(0, T, CHUNK)]
+
+        def term(u, r):
+            nb, t0 = units[u]
+            toks = slice(t0, t0 + CHUNK)
+            prod = work.tile([P, CHUNK], F32, name=f"term{r}", bufs=2)
+            picked = y[nb][:].indirect(lists[r][:, t0 // 16 : (t0 + CHUNK) // 16])
+            if r == 0 and u % 2 == 0:
+                nc.vector.tensor_tensor(prod[:], picked, gates[r][:, toks], MULT)
+            else:
+                plain = work.tile([P, CHUNK], F32, name="plain", bufs=6)
+                nc.scalar.activation(plain[:], picked, COPY)
+                nc.vector.tensor_tensor(prod[:], plain[:], gates[r][:, toks], MULT)
+            return prod
+
+        first = term(0, 0)
+        for u, (nb, t0) in enumerate(units):
+            second = term(u, 1)
+            third = term(u, 2)
+            part = work.tile([P, CHUNK], F32, name="part", bufs=2)
+            nc.vector.tensor_tensor(part[:], first[:], second[:], ADD)
+            if u + 1 < len(units):
+                first = term(u + 1, 0)
+            res = work.tile([P, CHUNK], F32, name="res", bufs=4)
+            nc.vector.tensor_tensor(res[:], part[:], third[:], ADD)
+            nc.sync.dma_start(out[nb * P : (nb + 1) * P, t0 : t0 + CHUNK], res[:])

@@ -25,11 +25,9 @@ SIGMOID = mybir.ActivationFunctionType.Sigmoid
 P = 128
 PACK = 4
 HALF = 128
-W2_LAG = 3
 CHUNK = 512
-V_M1 = 128
-V_M3 = 0
-V_C2 = 128
+W1_ON_SCALAR = 2
+W2_ON_SCALAR = 5
 
 
 def tile_moe_ecr_glu_sigmoid_kernel(tc, x_words, x_scales, w1, w3, w2, gate, offs, pos1, pos2, pos3, out):
@@ -42,10 +40,10 @@ def tile_moe_ecr_glu_sigmoid_kernel(tc, x_words, x_scales, w1, w3, w2, gate, off
 
         offs_sb = keep.tile([P, S // 16], U16, name="offs_sb")
         nc.sync.dma_start(offs_sb[:], offs)
-        xw = keep.tile([P, T], I32, name="xw", align_bytes=64)
-        nc.sync.dma_start(xw[:], x_words[0].rearrange("p t r -> p (t r)").bitcast(I32))
         xs_rows = keep.tile([4, 4, T // 4], I32, name="xs_rows")
         nc.sync.dma_start(xs_rows[:], x_scales[0].bitcast(I32).rearrange("(q r) w -> r q w", r=4))
+        xw = keep.tile([P, T], I32, name="xw", align_bytes=64)
+        nc.sync.dma_start(xw[:], x_words[0].rearrange("p t r -> p (t r)").bitcast(I32))
         xs = keep.tile([P, T], U8, name="xs", align_bytes=64)
         nc.vector.memset(xs[:].bitcast(I32), 0)
         for q in range(4):
@@ -60,26 +58,26 @@ def tile_moe_ecr_glu_sigmoid_kernel(tc, x_words, x_scales, w1, w3, w2, gate, off
 
         def gather_tokens(pair):
             cols = offs_sb[:, pair * 2 * C // 16 : (pair + 1) * 2 * C // 16]
-            xg_words[pair] = work.tile([P, 2 * C], U32, name="xgw", align_bytes=64)
-            xg_scales[pair] = work.tile([P, 2 * C], U8, name="xgs", align_bytes=64)
+            xg_words[pair] = work.tile([P, 2 * C], U32, name="xgw", align_bytes=64, bufs=E // 2)
+            xg_scales[pair] = work.tile([P, 2 * C], U8, name="xgs", align_bytes=64, bufs=E // 2)
             nc.vector.tensor_copy(xg_words[pair][:], xw[:].bitcast(U32).indirect(cols))
             nc.vector.tensor_copy(xg_scales[pair][:], xs[:].indirect(cols))
 
-        def load_first(w, e, name):
+        def load_first(w, e, name, in_halves=False):
             rows = w[e].rearrange("(p j) c -> p j c", j=PACK)
-            if e > 0:
-                t = raw.tile([P, PACK, H], F32, name=name, tag="raw13", bufs=10)
+            if not in_halves:
+                t = raw.tile([P, PACK, H], F32, name=name, tag="raw13", bufs=8)
                 nc.sync.dma_start(t[:], rows)
                 return [t]
             parts = []
             for c0 in range(0, H, N):
-                t = raw.tile([P, PACK, N], F32, name=name + "_part", tag="raw2", bufs=6)
+                t = raw.tile([P, PACK, N], F32, name=name + "_part", tag="raw13", bufs=8)
                 nc.sync.dma_start(t[:], rows[:, :, c0 : c0 + N])
                 parts.append(t)
             return parts
 
         def load_second(e):
-            t = raw.tile([P, PACK, N], F32, name="w2_raw", tag="raw2", bufs=6)
+            t = raw.tile([P, PACK, N], F32, name="w2_raw", tag="raw2", bufs=E)
             nc.sync.dma_start(t[:], w2[e].rearrange("(p j) n -> p j n", j=PACK))
             return t
 
@@ -89,33 +87,22 @@ def tile_moe_ecr_glu_sigmoid_kernel(tc, x_words, x_scales, w1, w3, w2, gate, off
             nc.vector.quantize_mx(out=codes[:].bitcast(FP8X4), scales=scales[:], in_=src[:])
             return codes, scales
 
-        def round_first(w_raw, name, on_vector):
-            grouped = work.tile([P, PACK * H], BF16, name=name + "_bf", align_bytes=64)
-            dst = grouped[:].rearrange("p (t m j) -> p m j t", t=PACK, j=PACK)
-            if len(w_raw) > 1:
-                for i, part in enumerate(w_raw):
-                    m = P // len(w_raw)
-                    nc.scalar.copy(dst[:, i * m : (i + 1) * m], part[:].rearrange("p j (m t) -> p m j t", t=PACK))
-                return quantize(grouped, H, name, 2)
-            src = w_raw[0][:].rearrange("p j (m t) -> p m j t", t=PACK)
-            if on_vector > 0:
-                nc.vector.tensor_copy(dst[:, :on_vector], src[:, :on_vector])
-            if on_vector < P:
-                nc.scalar.copy(dst[:, on_vector:], src[:, on_vector:])
-            return quantize(grouped, H, name, 2)
+        def round_first(w_raw, grouped, copy):
+            dst = grouped.rearrange("p (t m j) -> p m j t", t=PACK, j=PACK)
+            m = P // len(w_raw)
+            for i, part in enumerate(w_raw):
+                copy(dst[:, i * m : (i + 1) * m], part[:].rearrange("p j (m t) -> p m j t", t=PACK))
 
-        def first_layer(e, w1_raw, w3_raw):
-            w3q = round_first(w3_raw, "w3", V_M3)
-            w1q = round_first(w1_raw, "w1", V_M1)
-            h = work.tile([P, C * PACK], BF16, name="h", align_bytes=64)
+        def first_layer(e, grouped, h):
+            codes, scales = quantize(grouped, 2 * H, "w13", 2)
             for half in range(C // HALF):
                 first = (e % 2) * C + half * HALF
                 slots = slice(first, first + HALF)
                 banks = []
-                for name, (codes, scales) in (("a", w1q), ("b", w3q)):
+                for name, col0 in (("a", 0), ("b", H)):
                     bank = psum.tile([P, PACK, HALF], F32, name=name, bufs=3)
                     for t in range(PACK):
-                        cols = slice(t * P, (t + 1) * P)
+                        cols = slice(col0 + t * P, col0 + (t + 1) * P)
                         nc.tensor.matmul_mx(
                             out=bank[:, t, :],
                             lhsT=codes[:, cols].bitcast(FP8X4),
@@ -128,17 +115,18 @@ def tile_moe_ecr_glu_sigmoid_kernel(tc, x_words, x_scales, w1, w3, w2, gate, off
                     banks.append(bank)
                 sig = work.tile([P, HALF, PACK], F32, name="sig", bufs=3)
                 nc.scalar.activation(sig[:], banks[0][:].rearrange("p t n -> p n t"), SIGMOID)
-                h_half = h[:, half * HALF * PACK : (half + 1) * HALF * PACK].rearrange("p (n t) -> p n t", t=PACK)
+                h_half = h[:, first * PACK : (first + HALF) * PACK].rearrange("p (n t) -> p n t", t=PACK)
                 nc.vector.tensor_tensor(h_half, banks[1][:].rearrange("p t n -> p n t"), sig[:], MULT)
-            return quantize(h, C, "h", W2_LAG + 2)
 
         def second_layer(e, w2_raw, hq):
-            grouped = work.tile([P, PACK * N], BF16, name="w2_bf", align_bytes=64)
-            src = w2_raw[:].rearrange("p j (c i) -> p c j i", i=4)
-            cut = V_C2 * PACK
-            nc.vector.tensor_copy(grouped[:, :cut].rearrange("p (c i j) -> p c j i", i=4, j=PACK), src[:, : V_C2 // 4])
-            nc.scalar.copy(grouped[:, cut:].rearrange("p (c i j) -> p c j i", i=4, j=PACK), src[:, V_C2 // 4 :])
-            codes, scales = quantize(grouped, N, "w2", 2)
+            grouped = work.tile([P, PACK * N], BF16, name="w2_bf", align_bytes=64, bufs=3)
+            copy = nc.scalar.copy if e < W2_ON_SCALAR else nc.vector.tensor_copy
+            copy(
+                grouped[:].rearrange("p (c i j) -> p c j i", i=4, j=PACK),
+                w2_raw[:].rearrange("p j (c i) -> p c j i", i=4),
+            )
+            codes, scales = quantize(grouped, N, "w2", 3)
+            slots = slice((e % 2) * C, (e % 2 + 1) * C)
             bank = psum.tile([P, N // P, C], F32, name="ybank", bufs=2)
             for nb in range(N // P):
                 cols = slice(nb * P, (nb + 1) * P)
@@ -146,28 +134,36 @@ def tile_moe_ecr_glu_sigmoid_kernel(tc, x_words, x_scales, w1, w3, w2, gate, off
                     out=bank[:, nb, :],
                     lhsT=codes[:, cols].bitcast(FP8X4),
                     lhsT_scale=scales[:, cols],
-                    rhs=hq[0][:].bitcast(FP8X4),
-                    rhs_scale=hq[1][:],
+                    rhs=hq[0][:, slots].bitcast(FP8X4),
+                    rhs_scale=hq[1][:, slots],
                     start=True,
                     stop=True,
                 )
             for nb in range(N // P):
                 nc.scalar.copy(y[nb][:, e * C : (e + 1) * C], bank[:, nb, :])
 
-        hq = {}
-        for step in range(E + W2_LAG):
-            e2 = step - W2_LAG
-            if step < E:
-                w3_raw = load_first(w3, step, "w3_raw")
-                w1_raw = load_first(w1, step, "w1_raw")
-            if e2 >= 0:
-                w2_raw = load_second(e2)
-            if step < E:
-                if step % 2 == 0:
-                    gather_tokens(step // 2)
-                hq[step] = first_layer(step, w1_raw, w3_raw)
-            if e2 >= 0:
-                second_layer(e2, w2_raw, hq[e2])
+        hq = []
+        for pair in range(E // 2):
+            h = work.tile([P, 2 * C * PACK], BF16, name="h", align_bytes=64)
+            experts = (2 * pair, 2 * pair + 1)
+            order = [(w, e) for w in (3, 1) for e in experts] if pair == 0 else [(w, e) for e in experts for w in (3, 1)]
+            loaded = {}
+            for w, e in order:
+                loaded[w, e] = load_first(w3 if w == 3 else w1, e, "w13_raw", in_halves=(w, e) == (3, 0))
+            gather_tokens(pair)
+            grouped = {}
+            for w, e in order:
+                if e not in grouped:
+                    grouped[e] = work.tile([P, 2 * PACK * H], BF16, name="w13_bf", align_bytes=64, bufs=3)
+                if w == 3:
+                    round_first(loaded[w, e], grouped[e][:, PACK * H :], nc.scalar.copy)
+                else:
+                    round_first(loaded[w, e], grouped[e][:, : PACK * H], nc.scalar.copy if e < W1_ON_SCALAR else nc.vector.tensor_copy)
+            for e in experts:
+                first_layer(e, grouped[e], h)
+            hq.append(quantize(h, 2 * C, "h", E // 2))
+        for e in range(E):
+            second_layer(e, load_second(e), hq[e // 2])
 
         lists = []
         gates = []
@@ -175,7 +171,7 @@ def tile_moe_ecr_glu_sigmoid_kernel(tc, x_words, x_scales, w1, w3, w2, gate, off
             pos_sb = keep.tile([P, T // 16], U16, name=f"pos{r}")
             nc.sync.dma_start(pos_sb[:], pos)
             lists.append(pos_sb)
-            g = raw.tile([P, T], F32, name=f"gate{r}", tag="raw2", bufs=6)
+            g = raw.tile([P, T], F32, name=f"gate{r}", tag="raw13", bufs=8)
             nc.sync.dma_start(g[:], gate[r, 0:P, :])
             gates.append(g)
 
@@ -189,7 +185,7 @@ def tile_moe_ecr_glu_sigmoid_kernel(tc, x_words, x_scales, w1, w3, w2, gate, off
             if r == 0 and u % 2 == 0:
                 nc.vector.tensor_tensor(prod[:], picked, gates[r][:, toks], MULT)
             else:
-                plain = work.tile([P, CHUNK], F32, name="plain", bufs=6)
+                plain = work.tile([P, CHUNK], F32, name="plain", bufs=4)
                 nc.scalar.activation(plain[:], picked, COPY)
                 nc.vector.tensor_tensor(prod[:], plain[:], gates[r][:, toks], MULT)
             return prod
@@ -202,6 +198,6 @@ def tile_moe_ecr_glu_sigmoid_kernel(tc, x_words, x_scales, w1, w3, w2, gate, off
             nc.vector.tensor_tensor(part[:], first[:], second[:], ADD)
             if u + 1 < len(units):
                 first = term(u + 1, 0)
-            res = work.tile([P, CHUNK], F32, name="res", bufs=4)
+            res = work.tile([P, CHUNK], F32, name="res", bufs=3)
             nc.vector.tensor_tensor(res[:], part[:], third[:], ADD)
             nc.sync.dma_start(out[nb * P : (nb + 1) * P, t0 : t0 + CHUNK], res[:])

@@ -26,7 +26,7 @@ P = 128
 PACK = 4
 HALF = 128
 CHUNK = 512
-W1_ON_SCALAR = 2
+W1_ON_SCALAR = 1
 W2_ON_SCALAR = 5
 
 
@@ -88,10 +88,10 @@ def tile_moe_ecr_glu_sigmoid_kernel(tc, x_words, x_scales, w1, w3, w2, gate, off
             return codes, scales
 
         def round_first(w_raw, grouped, copy):
-            dst = grouped.rearrange("p (t m j) -> p m j t", t=PACK, j=PACK)
+            dst = grouped.rearrange("p (u v m j) -> p u m j v", u=2, v=2, j=PACK)
             m = P // len(w_raw)
             for i, part in enumerate(w_raw):
-                copy(dst[:, i * m : (i + 1) * m], part[:].rearrange("p j (m t) -> p m j t", t=PACK))
+                copy(dst[:, :, i * m : (i + 1) * m], part[:].rearrange("p j (m u v) -> p u m j v", u=2, v=2))
 
         def first_layer(e, grouped, h):
             codes, scales = quantize(grouped, 2 * H, "w13", 2)
@@ -122,8 +122,8 @@ def tile_moe_ecr_glu_sigmoid_kernel(tc, x_words, x_scales, w1, w3, w2, gate, off
             grouped = work.tile([P, PACK * N], BF16, name="w2_bf", align_bytes=64, bufs=3)
             copy = nc.scalar.copy if e < W2_ON_SCALAR else nc.vector.tensor_copy
             copy(
-                grouped[:].rearrange("p (c i j) -> p c j i", i=4, j=PACK),
-                w2_raw[:].rearrange("p j (c i) -> p c j i", i=4),
+                grouped[:].rearrange("p (c i j) -> p c j i", i=2, j=PACK),
+                w2_raw[:].rearrange("p j (c i) -> p c j i", i=2),
             )
             codes, scales = quantize(grouped, N, "w2", 3)
             slots = slice((e % 2) * C, (e % 2 + 1) * C)

@@ -24,21 +24,28 @@ SIGMOID = mybir.ActivationFunctionType.Sigmoid
 
 P = 128
 PACK = 4
-HALF = 128
+LIST_ROWS = 16
+PAIR = 2 * C
+BANK_SLOTS = 128
 CHUNK = 512
+
 W1_ON_SCALAR = 1
 W2_ON_SCALAR = 5
+W2_LAG = 5
+LOAD_RING = 12
 
 
-def tile_moe_ecr_glu_sigmoid_kernel(tc, x_words, x_scales, w1, w3, w2, gate, offs, pos1, pos2, pos3, out):
+def tile_moe_ecr_glu_sigmoid_kernel(
+    tc, x_words, x_scales, w1, w3, w2, gate, offs, pos1, pos2, pos3, out
+):
     nc = tc.nc
     with ExitStack() as ctx:
         keep = ctx.enter_context(tc.tile_pool(name="keep", bufs=1))
-        raw = ctx.enter_context(tc.tile_pool(name="raw", bufs=1))
+        raw = ctx.enter_context(tc.tile_pool(name="raw", bufs=LOAD_RING))
         work = ctx.enter_context(tc.tile_pool(name="work", bufs=2))
         psum = ctx.enter_context(tc.psum_pool(name="psum", bufs=1))
 
-        offs_sb = keep.tile([P, S // 16], U16, name="offs_sb")
+        offs_sb = keep.tile([P, S // LIST_ROWS], U16, name="offs_sb")
         nc.sync.dma_start(offs_sb[:], offs)
         xs_rows = keep.tile([4, 4, T // 4], I32, name="xs_rows")
         nc.sync.dma_start(xs_rows[:], x_scales[0].bitcast(I32).rearrange("(q r) w -> r q w", r=4))
@@ -53,151 +60,143 @@ def tile_moe_ecr_glu_sigmoid_kernel(tc, x_words, x_scales, w1, w3, w2, gate, off
         for nb in range(N // P):
             nc.gpsimd.memset(y[nb][:, S:], 0.0)
 
-        xg_words = {}
-        xg_scales = {}
-
         def gather_tokens(pair):
-            cols = offs_sb[:, pair * 2 * C // 16 : (pair + 1) * 2 * C // 16]
-            xg_words[pair] = work.tile([P, 2 * C], U32, name="xgw", align_bytes=64, bufs=E // 2)
-            xg_scales[pair] = work.tile([P, 2 * C], U8, name="xgs", align_bytes=64, bufs=E // 2)
-            nc.vector.tensor_copy(xg_words[pair][:], xw[:].bitcast(U32).indirect(cols))
-            nc.vector.tensor_copy(xg_scales[pair][:], xs[:].indirect(cols))
+            entries = offs_sb[:, pair * PAIR // LIST_ROWS : (pair + 1) * PAIR // LIST_ROWS]
+            words = work.tile([P, PAIR], U32, name="xg_words", align_bytes=64, bufs=E // 2)
+            scales = work.tile([P, PAIR], U8, name="xg_scales", align_bytes=64, bufs=E // 2)
+            nc.vector.tensor_copy(words[:], xw[:].bitcast(U32).indirect(entries))
+            nc.vector.tensor_copy(scales[:], xs[:].indirect(entries))
+            return words, scales
 
-        def load_first(w, e, name, in_halves=False):
-            rows = w[e].rearrange("(p j) c -> p j c", j=PACK)
-            if not in_halves:
-                t = raw.tile([P, PACK, H], F32, name=name, tag="raw13", bufs=8)
-                nc.sync.dma_start(t[:], rows)
-                return [t]
-            parts = []
-            for c0 in range(0, H, N):
-                t = raw.tile([P, PACK, N], F32, name=name + "_part", tag="raw13", bufs=8)
-                nc.sync.dma_start(t[:], rows[:, :, c0 : c0 + N])
-                parts.append(t)
-            return parts
+        def load_weight(matrix, parts=1):
+            rows = matrix.rearrange("(p j) c -> p j c", j=PACK)
+            width = matrix.shape[1] // parts
+            tiles = []
+            for c0 in range(0, matrix.shape[1], width):
+                tile = raw.tile([P, PACK, width], F32, name="weight", tag="load")
+                nc.sync.dma_start(tile[:], rows[:, :, c0 : c0 + width])
+                tiles.append(tile)
+            return tiles
 
-        def load_second(e):
-            t = raw.tile([P, PACK, N], F32, name="w2_raw", tag="raw2", bufs=E)
-            nc.sync.dma_start(t[:], w2[e].rearrange("(p j) n -> p j n", j=PACK))
-            return t
-
-        def quantize(src, width, name, bufs):
-            codes = work.tile([P, width], U32, name=name + "_codes", align_bytes=64, bufs=bufs)
+        def quantize(name, rounded, bufs):
+            width = rounded.shape[1] // PACK
+            words = work.tile([P, width], U32, name=name + "_words", align_bytes=64, bufs=bufs)
             scales = work.tile([P, width], U8, name=name + "_scales", align_bytes=64, bufs=bufs)
-            nc.vector.quantize_mx(out=codes[:].bitcast(FP8X4), scales=scales[:], in_=src[:])
-            return codes, scales
+            nc.vector.quantize_mx(out=words[:].bitcast(FP8X4), scales=scales[:], in_=rounded[:])
+            return words, scales
 
-        def round_first(w_raw, grouped, copy):
-            dst = grouped.rearrange("p (u v m j) -> p u m j v", u=2, v=2, j=PACK)
-            m = P // len(w_raw)
-            for i, part in enumerate(w_raw):
-                copy(dst[:, :, i * m : (i + 1) * m], part[:].rearrange("p j (m u v) -> p u m j v", u=2, v=2))
+        def matmul(bank, weights, w_cols, moving, m_cols):
+            nc.tensor.matmul_mx(
+                out=bank,
+                lhsT=weights[0][:, w_cols].bitcast(FP8X4),
+                lhsT_scale=weights[1][:, w_cols],
+                rhs=moving[0][:, m_cols].bitcast(FP8X4),
+                rhs_scale=moving[1][:, m_cols],
+                start=True,
+                stop=True,
+            )
 
-        def first_layer(e, grouped, h):
-            codes, scales = quantize(grouped, 2 * H, "w13", 2)
-            for half in range(C // HALF):
-                first = (e % 2) * C + half * HALF
-                slots = slice(first, first + HALF)
-                banks = []
-                for name, col0 in (("a", 0), ("b", H)):
-                    bank = psum.tile([P, PACK, HALF], F32, name=name, bufs=3)
-                    for t in range(PACK):
-                        cols = slice(col0 + t * P, col0 + (t + 1) * P)
-                        nc.tensor.matmul_mx(
-                            out=bank[:, t, :],
-                            lhsT=codes[:, cols].bitcast(FP8X4),
-                            lhsT_scale=scales[:, cols],
-                            rhs=xg_words[e // 2][:, slots].bitcast(FP8X4),
-                            rhs_scale=xg_scales[e // 2][:, slots],
-                            start=True,
-                            stop=True,
-                        )
-                    banks.append(bank)
-                sig = work.tile([P, HALF, PACK], F32, name="sig", bufs=3)
-                nc.scalar.activation(sig[:], banks[0][:].rearrange("p t n -> p n t"), SIGMOID)
-                h_half = h[:, first * PACK : (first + HALF) * PACK].rearrange("p (n t) -> p n t", t=PACK)
-                nc.vector.tensor_tensor(h_half, banks[1][:].rearrange("p t n -> p n t"), sig[:], MULT)
+        def round_first(parts, rounded, copy):
+            dst = rounded.rearrange("p (u v m j) -> p u m j v", u=2, v=2, j=PACK)
+            m = P // len(parts)
+            for n, part in enumerate(parts):
+                copy(dst[:, :, n * m : (n + 1) * m], part[:].rearrange("p j (m u v) -> p u m j v", u=2, v=2))
 
-        def second_layer(e, w2_raw, hq):
-            grouped = work.tile([P, PACK * N], BF16, name="w2_bf", align_bytes=64, bufs=3)
+        def first_layer(e, rounded, tokens, h):
+            w13 = quantize("w13", rounded, 2)
+            for s0 in range((e % 2) * C, (e % 2 + 1) * C, BANK_SLOTS):
+                slots = slice(s0, s0 + BANK_SLOTS)
+                a = psum.tile([P, PACK, BANK_SLOTS], F32, name="a", bufs=3)
+                for t in range(PACK):
+                    matmul(a[:, t, :], w13, slice(t * P, (t + 1) * P), tokens, slots)
+                b = psum.tile([P, PACK, BANK_SLOTS], F32, name="b", bufs=3)
+                for t in range(PACK):
+                    matmul(b[:, t, :], w13, slice(H + t * P, H + (t + 1) * P), tokens, slots)
+                sig = work.tile([P, BANK_SLOTS, PACK], F32, name="sig", bufs=3)
+                nc.scalar.activation(sig[:], a[:].rearrange("p t s -> p s t"), SIGMOID)
+                h_part = h[:, PACK * s0 : PACK * (s0 + BANK_SLOTS)].rearrange("p (s t) -> p s t", t=PACK)
+                nc.vector.tensor_tensor(h_part, b[:].rearrange("p t s -> p s t"), sig[:], MULT)
+
+        def second_layer(e, w2_raw, h_mx):
+            rounded = work.tile([P, PACK * N], BF16, name="w2_bf", align_bytes=64, bufs=3)
             copy = nc.scalar.copy if e < W2_ON_SCALAR else nc.vector.tensor_copy
             copy(
-                grouped[:].rearrange("p (c i j) -> p c j i", i=2, j=PACK),
-                w2_raw[:].rearrange("p j (c i) -> p c j i", i=2),
+                rounded[:].rearrange("p (c v j) -> p c j v", v=2, j=PACK),
+                w2_raw[:].rearrange("p j (c v) -> p c j v", v=2),
             )
-            codes, scales = quantize(grouped, N, "w2", 3)
-            slots = slice((e % 2) * C, (e % 2 + 1) * C)
+            w2_mx = quantize("w2", rounded, 3)
             bank = psum.tile([P, N // P, C], F32, name="ybank", bufs=2)
             for nb in range(N // P):
-                cols = slice(nb * P, (nb + 1) * P)
-                nc.tensor.matmul_mx(
-                    out=bank[:, nb, :],
-                    lhsT=codes[:, cols].bitcast(FP8X4),
-                    lhsT_scale=scales[:, cols],
-                    rhs=hq[0][:, slots].bitcast(FP8X4),
-                    rhs_scale=hq[1][:, slots],
-                    start=True,
-                    stop=True,
-                )
+                matmul(bank[:, nb, :], w2_mx, slice(nb * P, (nb + 1) * P), h_mx, slice((e % 2) * C, (e % 2 + 1) * C))
             for nb in range(N // P):
                 nc.scalar.copy(y[nb][:, e * C : (e + 1) * C], bank[:, nb, :])
 
-        hq = []
+        h_mx = []
         for pair in range(E // 2):
-            h = work.tile([P, 2 * C * PACK], BF16, name="h", align_bytes=64)
+            h = work.tile([P, PAIR * PACK], BF16, name="h", align_bytes=64)
             experts = (2 * pair, 2 * pair + 1)
-            order = [(w, e) for w in (3, 1) for e in experts] if pair == 0 else [(w, e) for e in experts for w in (3, 1)]
-            loaded = {}
-            for w, e in order:
-                loaded[w, e] = load_first(w3 if w == 3 else w1, e, "w13_raw", in_halves=(w, e) == (3, 0))
-            gather_tokens(pair)
-            grouped = {}
-            for w, e in order:
-                if e not in grouped:
-                    grouped[e] = work.tile([P, 2 * PACK * H], BF16, name="w13_bf", align_bytes=64, bufs=3)
-                if w == 3:
-                    round_first(loaded[w, e], grouped[e][:, PACK * H :], nc.scalar.copy)
+            if pair == 0:
+                order = [(is_w1, e) for is_w1 in (False, True) for e in experts]
+            else:
+                order = [(is_w1, e) for e in experts for is_w1 in (False, True)]
+            first_raw = {}
+            w2_raw = {}
+            for is_w1, e in order:
+                parts = 2 if (is_w1, e) == (False, 0) else 1
+                first_raw[is_w1, e] = load_weight((w1 if is_w1 else w3)[e], parts)
+                if is_w1 and e >= W2_LAG:
+                    w2_raw[e - W2_LAG] = load_weight(w2[e - W2_LAG])[0]
+            tokens = gather_tokens(pair)
+            rounded = {}
+            for is_w1, e in order:
+                if e not in rounded:
+                    rounded[e] = work.tile([P, 2 * PACK * H], BF16, name="w13_bf", align_bytes=64, bufs=3)
+                if is_w1:
+                    copy = nc.scalar.copy if e < W1_ON_SCALAR else nc.vector.tensor_copy
+                    round_first(first_raw[is_w1, e], rounded[e][:, : PACK * H], copy)
                 else:
-                    round_first(loaded[w, e], grouped[e][:, : PACK * H], nc.scalar.copy if e < W1_ON_SCALAR else nc.vector.tensor_copy)
+                    round_first(first_raw[is_w1, e], rounded[e][:, PACK * H :], nc.scalar.copy)
             for e in experts:
-                first_layer(e, grouped[e], h)
-            hq.append(quantize(h, 2 * C, "h", E // 2))
-        for e in range(E):
-            second_layer(e, load_second(e), hq[e // 2])
+                first_layer(e, rounded[e], tokens, h)
+                if e >= W2_LAG:
+                    second_layer(e - W2_LAG, w2_raw[e - W2_LAG], h_mx[(e - W2_LAG) // 2])
+            h_mx.append(quantize("h", h, E // 2))
+        for e in range(E - W2_LAG, E):
+            second_layer(e, load_weight(w2[e])[0], h_mx[e // 2])
 
         lists = []
         gates = []
         for r, pos in enumerate((pos1, pos2, pos3)):
-            pos_sb = keep.tile([P, T // 16], U16, name=f"pos{r}")
+            pos_sb = keep.tile([P, T // LIST_ROWS], U16, name=f"pos{r}")
             nc.sync.dma_start(pos_sb[:], pos)
             lists.append(pos_sb)
-            g = raw.tile([P, T], F32, name=f"gate{r}", tag="raw13", bufs=8)
-            nc.sync.dma_start(g[:], gate[r, 0:P, :])
-            gates.append(g)
+            gates.append(raw.tile([P, T], F32, name=f"gate{r}", tag="load"))
+        for t0 in range(0, T, CHUNK):
+            for r in range(TOP):
+                nc.sync.dma_start(gates[r][:, t0 : t0 + CHUNK], gate[r, 0:P, t0 : t0 + CHUNK])
 
-        units = [(nb, t0) for nb in range(N // P) for t0 in range(0, T, CHUNK)]
+        pieces = [(nb, t0) for nb in range(N // P) for t0 in range(0, T, CHUNK)]
 
-        def term(u, r):
-            nb, t0 = units[u]
-            toks = slice(t0, t0 + CHUNK)
-            prod = work.tile([P, CHUNK], F32, name=f"term{r}", bufs=2)
-            picked = y[nb][:].indirect(lists[r][:, t0 // 16 : (t0 + CHUNK) // 16])
-            if r == 0 and u % 2 == 0:
-                nc.vector.tensor_tensor(prod[:], picked, gates[r][:, toks], MULT)
+        def term(n, r):
+            nb, t0 = pieces[n]
+            product = work.tile([P, CHUNK], F32, name=f"term{r}")
+            picked = y[nb][:].indirect(lists[r][:, t0 // LIST_ROWS : (t0 + CHUNK) // LIST_ROWS])
+            if r == 0 and t0 == 0:
+                nc.vector.tensor_tensor(product[:], picked, gates[r][:, t0 : t0 + CHUNK], MULT)
             else:
                 plain = work.tile([P, CHUNK], F32, name="plain", bufs=4)
                 nc.scalar.activation(plain[:], picked, COPY)
-                nc.vector.tensor_tensor(prod[:], plain[:], gates[r][:, toks], MULT)
-            return prod
+                nc.vector.tensor_tensor(product[:], plain[:], gates[r][:, t0 : t0 + CHUNK], MULT)
+            return product
 
         first = term(0, 0)
-        for u, (nb, t0) in enumerate(units):
-            second = term(u, 1)
-            third = term(u, 2)
-            part = work.tile([P, CHUNK], F32, name="part", bufs=2)
-            nc.vector.tensor_tensor(part[:], first[:], second[:], ADD)
-            if u + 1 < len(units):
-                first = term(u + 1, 0)
-            res = work.tile([P, CHUNK], F32, name="res", bufs=3)
-            nc.vector.tensor_tensor(res[:], part[:], third[:], ADD)
-            nc.sync.dma_start(out[nb * P : (nb + 1) * P, t0 : t0 + CHUNK], res[:])
+        for n, (nb, t0) in enumerate(pieces):
+            second = term(n, 1)
+            third = term(n, 2)
+            partial = work.tile([P, CHUNK], F32, name="partial")
+            nc.vector.tensor_tensor(partial[:], first[:], second[:], ADD)
+            if n + 1 < len(pieces):
+                first = term(n + 1, 0)
+            total = work.tile([P, CHUNK], F32, name="total", bufs=3)
+            nc.vector.tensor_tensor(total[:], partial[:], third[:], ADD)
+            nc.sync.dma_start(out[nb * P : (nb + 1) * P, t0 : t0 + CHUNK], total[:])

@@ -181,7 +181,7 @@ def tile_moe_ecr_glu_sigmoid_kernel(
             nb, t0 = pieces[n]
             product = work.tile([P, CHUNK], F32, name=f"term{r}")
             picked = y[nb][:].indirect(lists[r][:, t0 // LIST_ROWS : (t0 + CHUNK) // LIST_ROWS])
-            if r == 0 and t0 == 0:
+            if r == 2 and t0 == 0:
                 nc.vector.tensor_tensor(product[:], picked, gates[r][:, t0 : t0 + CHUNK], MULT)
             else:
                 plain = work.tile([P, CHUNK], F32, name="plain", bufs=4)
@@ -189,14 +189,17 @@ def tile_moe_ecr_glu_sigmoid_kernel(
                 nc.vector.tensor_tensor(product[:], plain[:], gates[r][:, t0 : t0 + CHUNK], MULT)
             return product
 
-        first = term(0, 0)
+        third = term(0, 2)
         for n, (nb, t0) in enumerate(pieces):
+            first = term(n, 0)
             second = term(n, 1)
-            third = term(n, 2)
             partial = work.tile([P, CHUNK], F32, name="partial")
-            nc.vector.tensor_tensor(partial[:], first[:], second[:], ADD)
+            nc.vector.tensor_tensor(partial[:], third[:], first[:], ADD)
             if n + 1 < len(pieces):
-                first = term(n + 1, 0)
+                third = term(n + 1, 2)
             total = work.tile([P, CHUNK], F32, name="total", bufs=3)
-            nc.vector.tensor_tensor(total[:], partial[:], third[:], ADD)
-            nc.sync.dma_start(out[nb * P : (nb + 1) * P, t0 : t0 + CHUNK], total[:])
+            step = CHUNK if n + 1 < len(pieces) else CHUNK // 2
+            for c0 in range(0, CHUNK, step):
+                cols = slice(c0, c0 + step)
+                nc.vector.tensor_tensor(total[:, cols], partial[:, cols], second[:, cols], ADD)
+                nc.sync.dma_start(out[nb * P : (nb + 1) * P, t0 + c0 : t0 + c0 + step], total[:, cols])

from contextlib import ExitStack

import concourse.mybir as mybir

K, T, E, C, H, N = 512, 1024, 8, 256, 512, 256
TOP = 3
PAD = 64
S = E * C

FLOPS = 2 * S * (2 * K * H + H * N)
BYTES = 4 * E * (2 * K * H + H * N) + K * T + 16 * T + 4 * TOP * T + 2 * (S + TOP * T) + 4 * N * T

F32 = mybir.dt.float32
BF16 = mybir.dt.bfloat16
I32 = mybir.dt.int32
U32 = mybir.dt.uint32
U16 = mybir.dt.uint16
U8 = mybir.dt.uint8
FP8X4 = mybir.dt.float8_e4m3fn_x4
MULT = mybir.AluOpType.mult
ADD = mybir.AluOpType.add
COPY = mybir.ActivationFunctionType.Copy
SIGMOID = mybir.ActivationFunctionType.Sigmoid

P = 128
PACK = 4
LIST_ROWS = 16
PAIR = 2 * C
BANK_SLOTS = 128
CHUNK = 512

W1_ON_SCALAR = 1
W2_ON_SCALAR = 5
W2_LAG = 5
LOAD_RING = 12


def tile_moe_ecr_glu_sigmoid_kernel(
    tc, x_words, x_scales, w1, w3, w2, gate, offs, pos1, pos2, pos3, out
):
    nc = tc.nc
    with ExitStack() as ctx:
        keep = ctx.enter_context(tc.tile_pool(name="keep", bufs=1))
        raw = ctx.enter_context(tc.tile_pool(name="raw", bufs=LOAD_RING))
        work = ctx.enter_context(tc.tile_pool(name="work", bufs=2))
        psum = ctx.enter_context(tc.psum_pool(name="psum", bufs=1))

        offs_sb = keep.tile([P, S // LIST_ROWS], U16, name="offs_sb")
        nc.sync.dma_start(offs_sb[:], offs)
        xs_rows = keep.tile([4, 4, T // 4], I32, name="xs_rows")
        nc.sync.dma_start(xs_rows[:], x_scales[0].bitcast(I32).rearrange("(q r) w -> r q w", r=4))
        xw = keep.tile([P, T], I32, name="xw", align_bytes=64)
        nc.sync.dma_start(xw[:], x_words[0].rearrange("p t r -> p (t r)").bitcast(I32))
        xs = keep.tile([P, T], U8, name="xs", align_bytes=64)
        nc.vector.memset(xs[:].bitcast(I32), 0)
        for q in range(4):
            nc.vector.tensor_copy(xs[32 * q : 32 * q + 4, :].bitcast(I32), xs_rows[:, q, :])

        y = [keep.tile([P, S + PAD], F32, name=f"y{nb}") for nb in range(N // P)]
        for nb in range(N // P):
            nc.gpsimd.memset(y[nb][:, S:], 0.0)

        def gather_tokens(pair):
            entries = offs_sb[:, pair * PAIR // LIST_ROWS : (pair + 1) * PAIR // LIST_ROWS]
            words = work.tile([P, PAIR], U32, name="xg_words", align_bytes=64, bufs=E // 2)
            scales = work.tile([P, PAIR], U8, name="xg_scales", align_bytes=64, bufs=E // 2)
            nc.vector.tensor_copy(words[:], xw[:].bitcast(U32).indirect(entries))
            nc.vector.tensor_copy(scales[:], xs[:].indirect(entries))
            return words, scales

        def load_weight(matrix, parts=1):
            rows = matrix.rearrange("(p j) c -> p j c", j=PACK)
            width = matrix.shape[1] // parts
            tiles = []
            for c0 in range(0, matrix.shape[1], width):
                tile = raw.tile([P, PACK, width], F32, name="weight", tag="load")
                nc.sync.dma_start(tile[:], rows[:, :, c0 : c0 + width])
                tiles.append(tile)
            return tiles

        def quantize(name, rounded, bufs):
            width = rounded.shape[1] // PACK
            words = work.tile([P, width], U32, name=name + "_words", align_bytes=64, bufs=bufs)
            scales = work.tile([P, width], U8, name=name + "_scales", align_bytes=64, bufs=bufs)
            nc.vector.quantize_mx(out=words[:].bitcast(FP8X4), scales=scales[:], in_=rounded[:])
            return words, scales

        def matmul(bank, weights, w_cols, moving, m_cols):
            nc.tensor.matmul_mx(
                out=bank,
                lhsT=weights[0][:, w_cols].bitcast(FP8X4),
                lhsT_scale=weights[1][:, w_cols],
                rhs=moving[0][:, m_cols].bitcast(FP8X4),
                rhs_scale=moving[1][:, m_cols],
                start=True,
                stop=True,
            )

        def round_first(parts, rounded, copy):
            dst = rounded.rearrange("p (u v m j) -> p u m j v", u=2, v=2, j=PACK)
            m = P // len(parts)
            for n, part in enumerate(parts):
                copy(dst[:, :, n * m : (n + 1) * m], part[:].rearrange("p j (m u v) -> p u m j v", u=2, v=2))

        def first_layer(e, rounded, tokens, h):
            w13 = quantize("w13", rounded, 2)
            for s0 in range((e % 2) * C, (e % 2 + 1) * C, BANK_SLOTS):
                slots = slice(s0, s0 + BANK_SLOTS)
                a = psum.tile([P, PACK, BANK_SLOTS], F32, name="a", bufs=3)
                for t in range(PACK):
                    matmul(a[:, t, :], w13, slice(t * P, (t + 1) * P), tokens, slots)
                b = psum.tile([P, PACK, BANK_SLOTS], F32, name="b", bufs=3)
                for t in range(PACK):
                    matmul(b[:, t, :], w13, slice(H + t * P, H + (t + 1) * P), tokens, slots)
                sig = work.tile([P, BANK_SLOTS, PACK], F32, name="sig", bufs=3)
                nc.scalar.activation(sig[:], a[:].rearrange("p t s -> p s t"), SIGMOID)
                h_part = h[:, PACK * s0 : PACK * (s0 + BANK_SLOTS)].rearrange("p (s t) -> p s t", t=PACK)
                nc.vector.tensor_tensor(h_part, b[:].rearrange("p t s -> p s t"), sig[:], MULT)

        def second_layer(e, w2_raw, h_mx):
            rounded = work.tile([P, PACK * N], BF16, name="w2_bf", align_bytes=64, bufs=3)
            copy = nc.scalar.copy if e < W2_ON_SCALAR else nc.vector.tensor_copy
            copy(
                rounded[:].rearrange("p (c v j) -> p c j v", v=2, j=PACK),
                w2_raw[:].rearrange("p j (c v) -> p c j v", v=2),
            )
            w2_mx = quantize("w2", rounded, 3)
            bank = psum.tile([P, N // P, C], F32, name="ybank", bufs=2)
            for nb in range(N // P):
                matmul(bank[:, nb, :], w2_mx, slice(nb * P, (nb + 1) * P), h_mx, slice((e % 2) * C, (e % 2 + 1) * C))
            for nb in range(N // P):
                nc.scalar.copy(y[nb][:, e * C : (e + 1) * C], bank[:, nb, :])

        h_mx = []
        for pair in range(E // 2):
            h = work.tile([P, PAIR * PACK], BF16, name="h", align_bytes=64)
            experts = (2 * pair, 2 * pair + 1)
            if pair == 0:
                order = [(is_w1, e) for is_w1 in (False, True) for e in experts]
            else:
                order = [(is_w1, e) for e in experts for is_w1 in (False, True)]
            first_raw = {}
            w2_raw = {}
            for is_w1, e in order:
                parts = 2 if (is_w1, e) == (False, 0) else 1
                first_raw[is_w1, e] = load_weight((w1 if is_w1 else w3)[e], parts)
                if is_w1 and e >= W2_LAG:
                    w2_raw[e - W2_LAG] = load_weight(w2[e - W2_LAG])[0]
            tokens = gather_tokens(pair)
            rounded = {}
            for is_w1, e in order:
                if e not in rounded:
                    rounded[e] = work.tile([P, 2 * PACK * H], BF16, name="w13_bf", align_bytes=64, bufs=3)
                if is_w1:
                    copy = nc.scalar.copy if e < W1_ON_SCALAR else nc.vector.tensor_copy
                    round_first(first_raw[is_w1, e], rounded[e][:, : PACK * H], copy)
                else:
                    round_first(first_raw[is_w1, e], rounded[e][:, PACK * H :], nc.scalar.copy)
            for e in experts:
                first_layer(e, rounded[e], tokens, h)
                if e >= W2_LAG:
                    second_layer(e - W2_LAG, w2_raw[e - W2_LAG], h_mx[(e - W2_LAG) // 2])
            h_mx.append(quantize("h", h, E // 2))
        for e in range(E - W2_LAG, E):
            second_layer(e, load_weight(w2[e])[0], h_mx[e // 2])

        lists = []
        gates = []
        for r, pos in enumerate((pos1, pos2, pos3)):
            pos_sb = keep.tile([P, T // LIST_ROWS], U16, name=f"pos{r}")
            nc.sync.dma_start(pos_sb[:], pos)
            lists.append(pos_sb)
            gates.append(raw.tile([P, T], F32, name=f"gate{r}", tag="load"))
        for t0 in range(0, T, CHUNK):
            for r in range(TOP):
                nc.sync.dma_start(gates[r][:, t0 : t0 + CHUNK], gate[r, 0:P, t0 : t0 + CHUNK])

        pieces = [(nb, t0) for nb in range(N // P) for t0 in range(0, T, CHUNK)]

        def term(n, r):
            nb, t0 = pieces[n]
            product = work.tile([P, CHUNK], F32, name=f"term{r}")
            picked = y[nb][:].indirect(lists[r][:, t0 // LIST_ROWS : (t0 + CHUNK) // LIST_ROWS])
            if r == 2 and t0 == 0:
                nc.vector.tensor_tensor(product[:], picked, gates[r][:, t0 : t0 + CHUNK], MULT)
            else:
                plain = work.tile([P, CHUNK], F32, name="plain", bufs=4)
                nc.scalar.activation(plain[:], picked, COPY)
                nc.vector.tensor_tensor(product[:], plain[:], gates[r][:, t0 : t0 + CHUNK], MULT)
            return product

        third = term(0, 2)
        for n, (nb, t0) in enumerate(pieces):
            first = term(n, 0)
            second = term(n, 1)
            partial = work.tile([P, CHUNK], F32, name="partial")
            nc.vector.tensor_tensor(partial[:], third[:], first[:], ADD)
            if n + 1 < len(pieces):
                third = term(n + 1, 2)
            total = work.tile([P, CHUNK], F32, name="total", bufs=3)
            step = CHUNK if n + 1 < len(pieces) else CHUNK // 2
            for c0 in range(0, CHUNK, step):
                cols = slice(c0, c0 + step)
                nc.vector.tensor_tensor(total[:, cols], partial[:, cols], second[:, cols], ADD)
                nc.sync.dma_start(out[nb * P : (nb + 1) * P, t0 + c0 : t0 + c0 + step], total[:, cols])
